import numpy as np
import ml_dtypes


def mxq(x, axis, fmt="e4m3"):
    dtype, down = {"e4m3": (ml_dtypes.float8_e4m3fn, 7), "e5m2": (ml_dtypes.float8_e5m2, 14)}[fmt]
    v = np.moveaxis(np.asarray(x, np.float32).astype(ml_dtypes.bfloat16).astype(np.float64), axis, -1)
    blocks = v.reshape(v.shape[:-1] + (-1, 32))
    amax = np.abs(blocks).max(-1, keepdims=True)
    byte = np.maximum(np.where(amax > 0, np.frexp(amax)[1] - 1 + 127, 0) - down, 1)
    scale = np.exp2(byte - 127.0)
    codes = (blocks / scale).astype(np.float32).astype(dtype).astype(np.float64)
    return np.moveaxis((codes * scale).reshape(v.shape), -1, axis)


WIDE = False


def mx_kscale(k):
    if not WIDE:
        return np.ones(k)
    levels = np.array([10, -10, 5, -5, 0])
    if k % 512:
        return np.exp2(np.random.permutation(np.resize(levels, k // 32))).repeat(32)
    a = np.empty((k // 512, 16))
    for p in range(k // 512):
        a[p, :8] = np.random.permutation(np.resize(levels, 8))
        for g in range(8):
            far = levels[np.abs(levels - a[p, g]) >= 10]
            a[p, g + 8] = far[np.random.randint(len(far))]
    return np.exp2(a.ravel()).repeat(32)


def f64(x):
    return np.asarray(x).astype(np.float64)


def striped(idx):
    return np.tile(idx.reshape(-1, 16).T, (8, 1)).astype(np.uint16)


def unstriped(offs):
    return offs[:16].T.reshape(-1).astype(np.int64)


def striped8(idx):
    return np.concatenate([x.reshape(-1, 16).T for x in idx]).astype(np.uint16)


def runs(offs, k):
    lists = np.stack([offs[16 * r : 16 * r + 16].T.reshape(-1) for r in range(8)]).astype(np.int64)
    return lists[np.arange(k) % 512 // 64]


def pack_weight(w):
    k, n = w.shape
    w = f64(np.asarray(w, np.float32).astype(ml_dtypes.bfloat16)).reshape(k // 32, 32, n)
    amax = np.abs(w).max(1)
    byte = np.clip(np.where(amax > 0, np.frexp(amax)[1] - 1 + 127 - 7, 1), 1, 254)
    scaled = (w * np.exp2(127.0 - byte)[:, None, :]).reshape(k, n).astype(np.float32)
    words = np.ascontiguousarray(scaled.reshape(k // 512, 128, 4, n).transpose(0, 1, 3, 2)).astype(ml_dtypes.float8_e4m3fn).view(np.uint8)
    return words, np.ascontiguousarray(byte.astype(np.uint8).reshape(k // 512, 16, n))


def unpack_weight(words, scales):
    g, p, n, _ = words.shape
    vals = np.ascontiguousarray(words).view(ml_dtypes.float8_e4m3fn).astype(np.float64) * np.repeat(np.exp2(scales.astype(np.float64) - 127.0), 8, axis=1)[..., None]
    return vals.transpose(0, 1, 3, 2).reshape(g * 512, n)


K, T, S, N, G, H, W = 512, 2048, 256, 512, 2048, 512, 128


def setup_inputs():
    n = np.random.standard_normal
    s = mx_kscale(K)[:, None]
    u = mx_kscale(K)
    packed_xT = pack_weight(n((K, T)) * s)
    packed_dT = pack_weight(n((K, G)) / s)
    perm = np.random.permutation(S)
    perm2 = np.random.permutation(S)
    return {
        "x_words": packed_xT[0],
        "x_scales": packed_xT[1],
        "d_words": packed_dT[0],
        "d_scales": packed_dT[1],
        "gn": (np.random.uniform(0.5, 1.5, (H, 1)) * u[:, None]).astype(np.float32),
        "w1": (n((H, N)) / np.sqrt(H) / u[:, None]).astype(np.float32),
        "offs": striped8(np.random.randint(0, T, (8, S))),
        "k1": striped8(np.random.randint(0, G, (8, H))),
        "n1": striped(perm[:W]),
        "n2": striped(perm[W:]),
        "n3": striped(np.random.permutation(S)),
        "n4": striped(perm2[:W]),
        "n5": striped(perm2[W:]),
    }


def reference(x_words, x_scales, d_words, d_scales, gn, w1, offs, k1, n1, n2, n3, n4, n5):
    d_k1 = unpack_weight(d_words, d_scales)[np.arange(K)[:, None], runs(k1, K)]
    xq = unpack_weight(x_words, x_scales)[np.arange(K)[:, None], runs(offs, K)]
    h = 0.0625 * (d_k1.T @ xq)
    pa = h[:, unstriped(n1)]
    pb = h[:, unstriped(n2)]
    rb = np.minimum(pa, pb)
    ra = np.maximum(pa, pb)
    ds = np.zeros((H, S))
    ds[:, unstriped(n1)] = ra
    dt = ds.copy()
    dt[:, unstriped(n2)] = rb
    z = f64(gn) * (dt - dt[:, unstriped(n3)])
    h2 = mxq(f64(w1), 0, "e4m3").T @ mxq(z, 0, "e4m3")
    pa2 = h2[:, unstriped(n4)]
    pb2 = h2[:, unstriped(n5)]
    rb2 = pa2 - pb2
    ra2 = 0.75 * (pa2 + pb2)
    ds2 = np.zeros((N, S))
    ds2[:, unstriped(n4)] = ra2
    out = ds2.copy()
    out[:, unstriped(n5)] = rb2
    return out

@@ -1,0 +1,207 @@
+from contextlib import ExitStack
+
+import concourse.mybir as mybir
+
+K, T, S, N, G, H, W = 512, 2048, 256, 512, 2048, 512, 128
+FLOPS = 2 * K * H * S + 2 * H * N * S
+
+F32 = mybir.dt.float32
+BF16 = mybir.dt.bfloat16
+I32 = mybir.dt.int32
+U32 = mybir.dt.uint32
+U16 = mybir.dt.uint16
+U8 = mybir.dt.uint8
+FP8X4 = mybir.dt.float8_e4m3fn_x4
+ALU = mybir.AluOpType
+COPY = mybir.ActivationFunctionType.Copy
+
+P = 128
+PACK = 4
+HALF = S // 2
+
+
+def tile_picked_hpqorddhaar_none_p_kernel(
+    tc, x_words, x_scales, d_words, d_scales, gn, w1, offs, k1, n1, n2, n3, n4, n5, out
+):
+    nc = tc.nc
+    with ExitStack() as ctx:
+        lists = ctx.enter_context(tc.tile_pool(name="lists", bufs=1))
+        keep = ctx.enter_context(tc.tile_pool(name="keep", bufs=1))
+        psum = ctx.enter_context(tc.psum_pool(name="psum", bufs=1))
+
+        def load_list(name, ap):
+            t = lists.tile(list(ap.shape), U16, name=name)
+            nc.sync.dma_start(t[:], ap)
+            return t
+
+        d_scale_table = keep.tile([P, G], U8, align_bytes=64)
+        x_scale_table = keep.tile([P, T], U8, align_bytes=64)
+        planes = keep.tile([P, H + S], U8, align_bytes=64)
+        nc.vector.memset(d_scale_table[:].bitcast(I32), 0)
+        nc.vector.memset(x_scale_table[:].bitcast(I32), 0)
+        nc.vector.memset(planes[:].bitcast(I32), 0)
+
+        k1_t = load_list("k1_t", k1)
+        offs_t = load_list("offs_t", offs)
+        d_table = keep.tile([P, G], I32, align_bytes=64)
+        x_table = keep.tile([P, T], I32, align_bytes=64, tag="x_then_w")
+        nc.sync.dma_start(d_table[:], d_words[0].rearrange("p n t -> p (n t)").bitcast(I32))
+        nc.sync.dma_start(x_table[:], x_words[0].rearrange("p n t -> p (n t)").bitcast(I32))
+        nc.scalar.dma_start(d_scale_table[:].bitcast(I32)[0:P:8, :], d_scales[0].bitcast(I32))
+        nc.scalar.dma_start(x_scale_table[:].bitcast(I32)[0:P:8, :], x_scales[0].bitcast(I32))
+        n1_t = load_list("n1_t", n1)
+        n2_t = load_list("n2_t", n2)
+        n3_t = load_list("n3_t", n3)
+        gain = keep.tile([P, PACK], F32)
+        nc.sync.dma_start(gain[:], gn.rearrange("(p t) o -> p (t o)", t=PACK))
+        n4_t = load_list("n4_t", n4)
+        n5_t = load_list("n5_t", n5)
+
+        picked_scales = keep.tile([P, H + S], U8, align_bytes=64)
+        nc.vector.tensor_copy(picked_scales[:, 0:H], d_scale_table[:].indirect(k1_t[:]))
+        nc.vector.tensor_copy(picked_scales[:, H:H + S], x_scale_table[:].indirect(offs_t[:]))
+        for j in range(4):
+            nc.scalar.dma_start(planes[:].bitcast(I32)[j:P:32, :], picked_scales[:].bitcast(I32)[8 * j:P:32, :])
+
+        d_picked = keep.tile([P, H], U32, align_bytes=64)
+        nc.vector.tensor_copy(d_picked[:], d_table[:].bitcast(U32).indirect(k1_t[:]))
+        d_dealt = keep.tile([P, H], U32, align_bytes=64)
+        nc.vector.tensor_copy(
+            d_dealt[:].rearrange("p (t b i) -> p b t i", t=PACK, i=4),
+            d_picked[:].rearrange("p (b i t) -> p b t i", t=PACK, i=4),
+        )
+        x_picked = keep.tile([P, S], U32, align_bytes=64)
+        nc.vector.tensor_copy(x_picked[:], x_table[:].bitcast(U32).indirect(offs_t[:]))
+        d_plane = keep.tile([P, H], U8, align_bytes=64)
+        nc.vector.tensor_copy(
+            d_plane[:].rearrange("p (t b i) -> p b t i", t=PACK, i=16),
+            planes[:, 0:H].rearrange("p (b i t) -> p b t i", t=PACK, i=16),
+        )
+
+        w_raw = keep.tile([P, PACK, N], F32, align_bytes=64, tag="x_then_w")
+        nc.sync.dma_start(w_raw[:], w1.rearrange("(p t) n -> p t n", t=PACK))
+
+        h = []
+        for t in range(PACK):
+            acc = psum.tile([P, S], F32, name="acc%d" % t, tag="bank%d" % t)
+            cols = slice(t * P, (t + 1) * P)
+            nc.tensor.matmul_mx(
+                out=acc[:], lhsT=d_dealt[:, cols].bitcast(FP8X4), lhsT_scale=d_plane[:, cols],
+                rhs=x_picked[:].bitcast(FP8X4), rhs_scale=planes[:, H:H + S], start=True, stop=True,
+            )
+            h_t = keep.tile([P, S], F32, name="h%d" % t)
+            nc.vector.tensor_scalar(h_t[:], acc[:], 0.0625, None, ALU.mult)
+            h.append(h_t)
+
+        def fetch_pair(name, window, first, second):
+            a = keep.tile([P, W], F32, name=name + "a")
+            b = keep.tile([P, W], F32, name=name + "b")
+            nc.scalar.activation(a[:], window[:].indirect(first[:]), COPY)
+            nc.scalar.activation(b[:], window[:].indirect(second[:]), COPY)
+            return a, b
+
+        ra, rb, dt = [], [], []
+        for t in range(PACK):
+            pa, pb = fetch_pair("p%d" % t, h[t], n1_t, n2_t)
+            ra_t = keep.tile([P, W], F32, name="ra%d" % t)
+            rb_t = keep.tile([P, W], F32, name="rb%d" % t)
+            nc.vector.tensor_tensor(ra_t[:], pa[:], pb[:], ALU.max)
+            nc.vector.tensor_tensor(rb_t[:], pa[:], pb[:], ALU.min)
+            ra.append(ra_t)
+            rb.append(rb_t)
+            dt.append(keep.tile([P, S], F32, name="dt%d" % t))
+
+        z_grouped = keep.tile([P, S, PACK], BF16, align_bytes=64)
+        other = [keep.tile([P, S], F32, name="other%d" % t) for t in range(PACK)]
+
+        def put_a(t):
+            nc.scalar.activation(dt[t][:].indirect(n1_t[:]), ra[t][:], COPY)
+
+        def put_b(t):
+            nc.scalar.activation(dt[t][:].indirect(n2_t[:]), rb[t][:], COPY)
+
+        def difference(t, half):
+            cols = slice(half * HALF, (half + 1) * HALF)
+            part = n3_t[:, half * HALF // 16:(half + 1) * HALF // 16]
+            nc.scalar.activation(other[t][:, cols], dt[t][:].indirect(part), COPY, scale=gain[:, t:t + 1])
+            nc.vector.scalar_tensor_tensor(
+                z_grouped[:, cols, t], dt[t][:, cols], gain[:, t:t + 1], other[t][:, cols], ALU.mult, ALU.subtract
+            )
+
+        w_codes = keep.tile([P, N], U32, align_bytes=64)
+        w_plane = keep.tile([P, N], U8, align_bytes=64)
+        w_grouped = keep.tile([P, N, PACK], BF16, align_bytes=64)
+
+        def round_w(m):
+            cols = slice(m * P, (m + 1) * P)
+            nc.vector.tensor_copy(
+                w_grouped[:, cols, :].rearrange("p (c i) t -> p c t i", i=4),
+                w_raw[:, :, cols].rearrange("p t (c i) -> p c t i", i=4),
+            )
+
+        def quantise_w(m):
+            cols = slice(m * P, (m + 1) * P)
+            nc.vector.quantize_mx(
+                out=w_codes[:, cols].bitcast(FP8X4), scales=w_plane[:, cols],
+                in_=w_grouped[:, cols, :].rearrange("p c t -> p (c t)"),
+            )
+
+        put_a(0)
+        put_a(1)
+        put_b(0)
+        put_b(1)
+        for m in range(PACK):
+            round_w(m)
+        for m in range(PACK):
+            quantise_w(m)
+        difference(0, 0)
+        difference(0, 1)
+        put_a(2)
+        difference(1, 0)
+        difference(1, 1)
+        put_b(2)
+        put_a(3)
+        difference(2, 0)
+        put_b(3)
+        difference(2, 1)
+
+        z_codes = keep.tile([P, S], U32, align_bytes=64)
+        z_plane = keep.tile([P, S], U8, align_bytes=64)
+        h2 = [keep.tile([P, S], F32, name="h2_%d" % m) for m in range(PACK)]
+        difference(3, 0)
+        difference(3, 1)
+        halves = [slice(0, HALF), slice(HALF, S)]
+        for cols in halves:
+            nc.vector.quantize_mx(
+                out=z_codes[:, cols].bitcast(FP8X4), scales=z_plane[:, cols],
+                in_=z_grouped[:, cols, :].rearrange("p c t -> p (c t)"),
+            )
+        for half, cols in enumerate(halves):
+            for m in range(PACK):
+                acc2 = psum.tile([P, HALF], F32, name="acc2_%d_%d" % (half, m), tag="bank%d" % (4 * (1 - half) + m))
+                rows = slice(m * P, (m + 1) * P)
+                nc.tensor.matmul_mx(
+                    out=acc2[:], lhsT=w_codes[:, rows].bitcast(FP8X4), lhsT_scale=w_plane[:, rows],
+                    rhs=z_codes[:, cols].bitcast(FP8X4), rhs_scale=z_plane[:, cols], start=True, stop=True,
+                )
+                if half == 0:
+                    nc.scalar.copy(h2[m][:, cols], acc2[:])
+                else:
+                    nc.vector.tensor_copy(h2[m][:, cols], acc2[:])
+
+        ra2, rb2, res = [], [], []
+        for m in range(PACK):
+            pa2, pb2 = fetch_pair("q%d" % m, h2[m], n4_t, n5_t)
+            ra2_m = keep.tile([P, W], F32, name="ra2_%d" % m)
+            rb2_m = keep.tile([P, W], F32, name="rb2_%d" % m)
+            nc.vector.tensor_tensor(ra2_m[:], pa2[:], pb2[:], ALU.add)
+            nc.vector.tensor_tensor(rb2_m[:], pa2[:], pb2[:], ALU.subtract)
+            ra2.append(ra2_m)
+            rb2.append(rb2_m)
+            res.append(keep.tile([P, S], F32, name="res%d" % m))
+        for m0 in (0, 2):
+            for m in (m0, m0 + 1):
+                nc.scalar.activation(res[m][:].indirect(n4_t[:]), ra2[m][:], COPY, scale=0.75)
+            for m in (m0, m0 + 1):
+                nc.scalar.activation(res[m][:].indirect(n5_t[:]), rb2[m][:], COPY)
+                nc.sync.dma_start(out[m * P:(m + 1) * P, :], res[m][:])

@@ -34,33 +34,34 @@ def tile_picked_hpqorddhaar_none_p_kernel(
             nc.sync.dma_start(t[:], ap)
             return t
 
-        d_scale_table = keep.tile([P, G], U8, align_bytes=64)
+        d_scale_table = keep.tile([P, G], U8, align_bytes=64, tag="scales_then_gain")
         x_scale_table = keep.tile([P, T], U8, align_bytes=64)
         planes = keep.tile([P, H + S], U8, align_bytes=64)
         nc.vector.memset(d_scale_table[:].bitcast(I32), 0)
-        nc.vector.memset(x_scale_table[:].bitcast(I32), 0)
-        nc.vector.memset(planes[:].bitcast(I32), 0)
+        nc.vector.memset(x_scale_table[:, 0:T // 2].bitcast(I32), 0)
+        nc.gpsimd.memset(x_scale_table[:, T // 2:T].bitcast(I32), 0)
 
         k1_t = load_list("k1_t", k1)
         offs_t = load_list("offs_t", offs)
-        d_table = keep.tile([P, G], I32, align_bytes=64)
-        x_table = keep.tile([P, T], I32, align_bytes=64, tag="x_then_w")
-        nc.sync.dma_start(d_table[:], d_words[0].rearrange("p n t -> p (n t)").bitcast(I32))
-        nc.sync.dma_start(x_table[:], x_words[0].rearrange("p n t -> p (n t)").bitcast(I32))
-        nc.scalar.dma_start(d_scale_table[:].bitcast(I32)[0:P:8, :], d_scales[0].bitcast(I32))
-        nc.scalar.dma_start(x_scale_table[:].bitcast(I32)[0:P:8, :], x_scales[0].bitcast(I32))
         n1_t = load_list("n1_t", n1)
         n2_t = load_list("n2_t", n2)
         n3_t = load_list("n3_t", n3)
-        gain = keep.tile([P, PACK], F32)
-        nc.sync.dma_start(gain[:], gn.rearrange("(p t) o -> p (t o)", t=PACK))
+        nc.sync.dma_start(d_scale_table[:].bitcast(I32)[0:P:8, :], d_scales[0].bitcast(I32))
+        nc.sync.dma_start(x_scale_table[:].bitcast(I32)[0:P:8, :], x_scales[0].bitcast(I32))
+        d_table = keep.tile([P, G], I32, align_bytes=64, tag="d_then_w")
+        x_table = keep.tile([P, T], I32, align_bytes=64, tag="x_then_plane")
+        nc.sync.dma_start(d_table[:], d_words[0].rearrange("p n t -> p (n t)").bitcast(I32))
+        nc.sync.dma_start(x_table[:], x_words[0].rearrange("p n t -> p (n t)").bitcast(I32))
         n4_t = load_list("n4_t", n4)
         n5_t = load_list("n5_t", n5)
 
         picked_scales = keep.tile([P, H + S], U8, align_bytes=64)
         nc.vector.tensor_copy(picked_scales[:, 0:H], d_scale_table[:].indirect(k1_t[:]))
         nc.vector.tensor_copy(picked_scales[:, H:H + S], x_scale_table[:].indirect(offs_t[:]))
-        for j in range(4):
+        gain = keep.tile([P, PACK], F32, align_bytes=64, tag="scales_then_gain")
+        nc.sync.dma_start(gain[:], gn.rearrange("(p t) o -> p (t o)", t=PACK))
+        nc.vector.tensor_copy(planes[:].bitcast(I32), picked_scales[:].bitcast(I32))
+        for j in range(1, 4):
             nc.scalar.dma_start(planes[:].bitcast(I32)[j:P:32, :], picked_scales[:].bitcast(I32)[8 * j:P:32, :])
 
         d_picked = keep.tile([P, H], U32, align_bytes=64)
@@ -72,13 +73,14 @@ def tile_picked_hpqorddhaar_none_p_kernel(
         )
         x_picked = keep.tile([P, S], U32, align_bytes=64)
         nc.vector.tensor_copy(x_picked[:], x_table[:].bitcast(U32).indirect(offs_t[:]))
-        d_plane = keep.tile([P, H], U8, align_bytes=64)
-        nc.vector.tensor_copy(
-            d_plane[:].rearrange("p (t b i) -> p b t i", t=PACK, i=16),
-            planes[:, 0:H].rearrange("p (b i t) -> p b t i", t=PACK, i=16),
-        )
+        d_plane = keep.tile([P, H], U8, align_bytes=64, tag="x_then_plane")
+        for slots in (slice(0, 1), slice(1, PACK)):
+            nc.vector.tensor_copy(
+                d_plane[:].rearrange("p (t b i) -> p b t i", t=PACK, i=16)[:, :, slots, :],
+                planes[:, 0:H].rearrange("p (b i t) -> p b t i", t=PACK, i=16)[:, :, slots, :],
+            )
 
-        w_raw = keep.tile([P, PACK, N], F32, align_bytes=64, tag="x_then_w")
+        w_raw = keep.tile([P, PACK, N], F32, align_bytes=64, tag="d_then_w")
         nc.sync.dma_start(w_raw[:], w1.rearrange("(p t) n -> p t n", t=PACK))
 
         h = []

@@ -41,6 +41,8 @@ def tile_picked_hpqorddhaar_none_p_kernel(
         nc.vector.memset(x_scale_table[:, 0:T // 2].bitcast(I32), 0)
         nc.gpsimd.memset(x_scale_table[:, T // 2:T].bitcast(I32), 0)
 
+        nc.vector.memset(planes[:].bitcast(I32), 0)
+
         k1_t = load_list("k1_t", k1)
         offs_t = load_list("offs_t", offs)
         n1_t = load_list("n1_t", n1)
@@ -49,7 +51,7 @@ def tile_picked_hpqorddhaar_none_p_kernel(
         nc.sync.dma_start(d_scale_table[:].bitcast(I32)[0:P:8, :], d_scales[0].bitcast(I32))
         nc.sync.dma_start(x_scale_table[:].bitcast(I32)[0:P:8, :], x_scales[0].bitcast(I32))
         d_table = keep.tile([P, G], I32, align_bytes=64, tag="d_then_w")
-        x_table = keep.tile([P, T], I32, align_bytes=64, tag="x_then_plane")
+        x_table = keep.tile([P, T], I32, align_bytes=64)
         nc.sync.dma_start(d_table[:], d_words[0].rearrange("p n t -> p (n t)").bitcast(I32))
         nc.sync.dma_start(x_table[:], x_words[0].rearrange("p n t -> p (n t)").bitcast(I32))
         n4_t = load_list("n4_t", n4)
@@ -60,9 +62,14 @@ def tile_picked_hpqorddhaar_none_p_kernel(
         nc.vector.tensor_copy(picked_scales[:, H:H + S], x_scale_table[:].indirect(offs_t[:]))
         gain = keep.tile([P, PACK], F32, align_bytes=64, tag="scales_then_gain")
         nc.sync.dma_start(gain[:], gn.rearrange("(p t) o -> p (t o)", t=PACK))
-        nc.vector.tensor_copy(planes[:].bitcast(I32), picked_scales[:].bitcast(I32))
-        for j in range(1, 4):
-            nc.scalar.dma_start(planes[:].bitcast(I32)[j:P:32, :], picked_scales[:].bitcast(I32)[8 * j:P:32, :])
+        dealt_scales = keep.tile([P, H + S], U8, align_bytes=64)
+        nc.vector.tensor_copy(
+            dealt_scales[:, 0:H].rearrange("p (t b i) -> p b t i", t=PACK, i=16),
+            picked_scales[:, 0:H].rearrange("p (b i t) -> p b t i", t=PACK, i=16),
+        )
+        nc.vector.tensor_copy(dealt_scales[:, H:H + S].bitcast(I32), picked_scales[:, H:H + S].bitcast(I32))
+        for j in range(4):
+            nc.scalar.dma_start(planes[:].bitcast(I32)[j:P:32, :], dealt_scales[:].bitcast(I32)[8 * j:P:32, :])
 
         d_picked = keep.tile([P, H], U32, align_bytes=64)
         nc.vector.tensor_copy(d_picked[:], d_table[:].bitcast(U32).indirect(k1_t[:]))
@@ -73,12 +80,6 @@ def tile_picked_hpqorddhaar_none_p_kernel(
         )
         x_picked = keep.tile([P, S], U32, align_bytes=64)
         nc.vector.tensor_copy(x_picked[:], x_table[:].bitcast(U32).indirect(offs_t[:]))
-        d_plane = keep.tile([P, H], U8, align_bytes=64, tag="x_then_plane")
-        for slots in (slice(0, 1), slice(1, PACK)):
-            nc.vector.tensor_copy(
-                d_plane[:].rearrange("p (t b i) -> p b t i", t=PACK, i=16)[:, :, slots, :],
-                planes[:, 0:H].rearrange("p (b i t) -> p b t i", t=PACK, i=16)[:, :, slots, :],
-            )
 
         w_raw = keep.tile([P, PACK, N], F32, align_bytes=64, tag="d_then_w")
         nc.sync.dma_start(w_raw[:], w1.rearrange("(p t) n -> p t n", t=PACK))
@@ -88,7 +89,7 @@ def tile_picked_hpqorddhaar_none_p_kernel(
             acc = psum.tile([P, S], F32, name="acc%d" % t, tag="bank%d" % t)
             cols = slice(t * P, (t + 1) * P)
             nc.tensor.matmul_mx(
-                out=acc[:], lhsT=d_dealt[:, cols].bitcast(FP8X4), lhsT_scale=d_plane[:, cols],
+                out=acc[:], lhsT=d_dealt[:, cols].bitcast(FP8X4), lhsT_scale=planes[:, cols],
                 rhs=x_picked[:].bitcast(FP8X4), rhs_scale=planes[:, H:H + S], start=True, stop=True,
             )
             h_t = keep.tile([P, S], F32, name="h%d" % t)
@@ -178,18 +179,18 @@ def tile_picked_hpqorddhaar_none_p_kernel(
                 out=z_codes[:, cols].bitcast(FP8X4), scales=z_plane[:, cols],
                 in_=z_grouped[:, cols, :].rearrange("p c t -> p (c t)"),
             )
-        for half, cols in enumerate(halves):
-            for m in range(PACK):
-                acc2 = psum.tile([P, HALF], F32, name="acc2_%d_%d" % (half, m), tag="bank%d" % (4 * (1 - half) + m))
-                rows = slice(m * P, (m + 1) * P)
-                nc.tensor.matmul_mx(
-                    out=acc2[:], lhsT=w_codes[:, rows].bitcast(FP8X4), lhsT_scale=w_plane[:, rows],
-                    rhs=z_codes[:, cols].bitcast(FP8X4), rhs_scale=z_plane[:, cols], start=True, stop=True,
-                )
-                if half == 0:
-                    nc.scalar.copy(h2[m][:, cols], acc2[:])
-                else:
-                    nc.vector.tensor_copy(h2[m][:, cols], acc2[:])
+        pieces = [(0, halves[0]), (0, halves[1])] + [(m, slice(0, S)) for m in range(1, PACK)]
+        for i, (m, cols) in enumerate(pieces):
+            acc2 = psum.tile([P, cols.stop - cols.start], F32, name="acc2_%d" % i, tag="bank%d" % ((i + PACK) % 8))
+            rows = slice(m * P, (m + 1) * P)
+            nc.tensor.matmul_mx(
+                out=acc2[:], lhsT=w_codes[:, rows].bitcast(FP8X4), lhsT_scale=w_plane[:, rows],
+                rhs=z_codes[:, cols].bitcast(FP8X4), rhs_scale=z_plane[:, cols], start=True, stop=True,
+            )
+            if i == 0:
+                nc.scalar.copy(h2[m][:, cols], acc2[:])
+            else:
+                nc.vector.tensor_copy(h2[m][:, cols], acc2[:])
 
         ra2, rb2, res = [], [], []
         for m in range(PACK):

@@ -17,7 +17,15 @@ COPY = mybir.ActivationFunctionType.Copy
 
 P = 128
 PACK = 4
-HALF = S // 2
+TILES = N // P
+LIST_ROWS = 16
+BLOCK_ROWS = 8
+QUADRANT = 32
+LINE_WORDS = 4
+BANKS = 8
+WHOLE = slice(0, S)
+HALVES = (slice(0, S // 2), slice(S // 2, S))
+PIECES = ((0, HALVES[0]), (0, HALVES[1]), (1, WHOLE), (2, WHOLE), (3, WHOLE))
 
 
 def tile_picked_hpqorddhaar_none_p_kernel(
@@ -30,9 +38,9 @@ def tile_picked_hpqorddhaar_none_p_kernel(
         psum = ctx.enter_context(tc.psum_pool(name="psum", bufs=1))
 
         def load_list(name, ap):
-            t = lists.tile(list(ap.shape), U16, name=name)
-            nc.sync.dma_start(t[:], ap)
-            return t
+            tile = lists.tile(list(ap.shape), U16, name=name)
+            nc.sync.dma_start(tile[:], ap)
+            return tile
 
         d_scale_table = keep.tile([P, G], U8, align_bytes=64, tag="scales_then_gain")
         x_scale_table = keep.tile([P, T], U8, align_bytes=64)
@@ -40,17 +48,16 @@ def tile_picked_hpqorddhaar_none_p_kernel(
         nc.vector.memset(d_scale_table[:].bitcast(I32), 0)
         nc.vector.memset(x_scale_table[:, 0:T // 2].bitcast(I32), 0)
         nc.gpsimd.memset(x_scale_table[:, T // 2:T].bitcast(I32), 0)
-
         nc.vector.memset(planes[:].bitcast(I32), 0)
 
         k1_t = load_list("k1_t", k1)
         offs_t = load_list("offs_t", offs)
         n1_t = load_list("n1_t", n1)
         n2_t = load_list("n2_t", n2)
+        nc.sync.dma_start(d_scale_table[:].bitcast(I32)[0:P:BLOCK_ROWS, :], d_scales[0].bitcast(I32))
         n3_t = load_list("n3_t", n3)
-        nc.sync.dma_start(d_scale_table[:].bitcast(I32)[0:P:8, :], d_scales[0].bitcast(I32))
-        nc.sync.dma_start(x_scale_table[:].bitcast(I32)[0:P:8, :], x_scales[0].bitcast(I32))
-        d_table = keep.tile([P, G], I32, align_bytes=64, tag="d_then_w")
+        nc.sync.dma_start(x_scale_table[:].bitcast(I32)[0:P:BLOCK_ROWS, :], x_scales[0].bitcast(I32))
+        d_table = keep.tile([P, G], I32, align_bytes=64, tag="words_then_w1")
         x_table = keep.tile([P, T], I32, align_bytes=64)
         nc.sync.dma_start(d_table[:], d_words[0].rearrange("p n t -> p (n t)").bitcast(I32))
         nc.sync.dma_start(x_table[:], x_words[0].rearrange("p n t -> p (n t)").bitcast(I32))
@@ -64,37 +71,38 @@ def tile_picked_hpqorddhaar_none_p_kernel(
         nc.sync.dma_start(gain[:], gn.rearrange("(p t) o -> p (t o)", t=PACK))
         dealt_scales = keep.tile([P, H + S], U8, align_bytes=64)
         nc.vector.tensor_copy(
-            dealt_scales[:, 0:H].rearrange("p (t b i) -> p b t i", t=PACK, i=16),
-            picked_scales[:, 0:H].rearrange("p (b i t) -> p b t i", t=PACK, i=16),
+            dealt_scales[:, 0:H].rearrange("p (t m) -> p t m", t=PACK),
+            picked_scales[:, 0:H].rearrange("p (m t) -> p t m", t=PACK),
         )
         nc.vector.tensor_copy(dealt_scales[:, H:H + S].bitcast(I32), picked_scales[:, H:H + S].bitcast(I32))
-        for j in range(4):
-            nc.scalar.dma_start(planes[:].bitcast(I32)[j:P:32, :], dealt_scales[:].bitcast(I32)[8 * j:P:32, :])
+        for j in range(QUADRANT // BLOCK_ROWS):
+            nc.scalar.dma_start(
+                planes[:].bitcast(I32)[j:P:QUADRANT, :], dealt_scales[:].bitcast(I32)[BLOCK_ROWS * j:P:QUADRANT, :]
+            )
 
         d_picked = keep.tile([P, H], U32, align_bytes=64)
         nc.vector.tensor_copy(d_picked[:], d_table[:].bitcast(U32).indirect(k1_t[:]))
         d_dealt = keep.tile([P, H], U32, align_bytes=64)
         nc.vector.tensor_copy(
-            d_dealt[:].rearrange("p (t b i) -> p b t i", t=PACK, i=4),
-            d_picked[:].rearrange("p (b i t) -> p b t i", t=PACK, i=4),
+            d_dealt[:].rearrange("p (t b i) -> p b t i", t=PACK, i=LINE_WORDS),
+            d_picked[:].rearrange("p (b i t) -> p b t i", t=PACK, i=LINE_WORDS),
         )
         x_picked = keep.tile([P, S], U32, align_bytes=64)
         nc.vector.tensor_copy(x_picked[:], x_table[:].bitcast(U32).indirect(offs_t[:]))
 
-        w_raw = keep.tile([P, PACK, N], F32, align_bytes=64, tag="d_then_w")
+        w_raw = keep.tile([P, PACK, N], F32, align_bytes=64, tag="words_then_w1")
         nc.sync.dma_start(w_raw[:], w1.rearrange("(p t) n -> p t n", t=PACK))
 
-        h = []
-        for t in range(PACK):
-            acc = psum.tile([P, S], F32, name="acc%d" % t, tag="bank%d" % t)
-            cols = slice(t * P, (t + 1) * P)
+        h = [keep.tile([P, S], F32, name="h%d" % t) for t in range(PACK)]
+        for i, (t, cols) in enumerate(PIECES):
+            acc = psum.tile([P, cols.stop - cols.start], F32, name="acc%d" % i, tag="bank%d" % i)
+            rows = slice(t * P, (t + 1) * P)
             nc.tensor.matmul_mx(
-                out=acc[:], lhsT=d_dealt[:, cols].bitcast(FP8X4), lhsT_scale=planes[:, cols],
-                rhs=x_picked[:].bitcast(FP8X4), rhs_scale=planes[:, H:H + S], start=True, stop=True,
+                out=acc[:], lhsT=d_dealt[:, rows].bitcast(FP8X4), lhsT_scale=planes[:, rows],
+                rhs=x_picked[:, cols].bitcast(FP8X4), rhs_scale=planes[:, H + cols.start:H + cols.stop],
+                start=True, stop=True,
             )
-            h_t = keep.tile([P, S], F32, name="h%d" % t)
-            nc.vector.tensor_scalar(h_t[:], acc[:], 0.0625, None, ALU.mult)
-            h.append(h_t)
+            nc.vector.tensor_scalar(h[t][:, cols], acc[:], 0.0625, None, ALU.mult)
 
         def fetch_pair(name, window, first, second):
             a = keep.tile([P, W], F32, name=name + "a")
@@ -112,99 +120,97 @@ def tile_picked_hpqorddhaar_none_p_kernel(
             nc.vector.tensor_tensor(rb_t[:], pa[:], pb[:], ALU.min)
             ra.append(ra_t)
             rb.append(rb_t)
-            dt.append(keep.tile([P, S], F32, name="dt%d" % t))
+            dt.append(keep.tile([P, 2 * S if t < PACK // 2 else S], F32, name="dt%d" % t))
 
         z_grouped = keep.tile([P, S, PACK], BF16, align_bytes=64)
-        other = [keep.tile([P, S], F32, name="other%d" % t) for t in range(PACK)]
+        partner = [keep.tile([P, S], F32, name="partner%d" % t) for t in range(PACK)]
 
-        def put_a(t):
+        def put_larger(t):
             nc.scalar.activation(dt[t][:].indirect(n1_t[:]), ra[t][:], COPY)
 
-        def put_b(t):
+        def put_smaller(t):
             nc.scalar.activation(dt[t][:].indirect(n2_t[:]), rb[t][:], COPY)
 
-        def difference(t, half):
-            cols = slice(half * HALF, (half + 1) * HALF)
-            part = n3_t[:, half * HALF // 16:(half + 1) * HALF // 16]
-            nc.scalar.activation(other[t][:, cols], dt[t][:].indirect(part), COPY, scale=gain[:, t:t + 1])
+        def make_z(t, cols):
+            entries = n3_t[:, cols.start // LIST_ROWS:cols.stop // LIST_ROWS]
+            nc.scalar.activation(partner[t][:, cols], dt[t][:].indirect(entries), COPY, scale=gain[:, t:t + 1])
             nc.vector.scalar_tensor_tensor(
-                z_grouped[:, cols, t], dt[t][:, cols], gain[:, t:t + 1], other[t][:, cols], ALU.mult, ALU.subtract
+                z_grouped[:, cols, t], dt[t][:, cols], gain[:, t:t + 1], partner[t][:, cols], ALU.mult, ALU.subtract
             )
 
         w_codes = keep.tile([P, N], U32, align_bytes=64)
         w_plane = keep.tile([P, N], U8, align_bytes=64)
         w_grouped = keep.tile([P, N, PACK], BF16, align_bytes=64)
 
-        def round_w(m):
-            cols = slice(m * P, (m + 1) * P)
+        def round_w(u):
+            cols = slice(u * P, (u + 1) * P)
             nc.vector.tensor_copy(
-                w_grouped[:, cols, :].rearrange("p (c i) t -> p c t i", i=4),
-                w_raw[:, :, cols].rearrange("p t (c i) -> p c t i", i=4),
+                w_grouped[:, cols, :].rearrange("p (c i) t -> p c t i", i=LINE_WORDS),
+                w_raw[:, :, cols].rearrange("p t (c i) -> p c t i", i=LINE_WORDS),
             )
 
-        def quantise_w(m):
-            cols = slice(m * P, (m + 1) * P)
+        def quantise_w(u):
+            cols = slice(u * P, (u + 1) * P)
             nc.vector.quantize_mx(
                 out=w_codes[:, cols].bitcast(FP8X4), scales=w_plane[:, cols],
                 in_=w_grouped[:, cols, :].rearrange("p c t -> p (c t)"),
             )
 
-        put_a(0)
-        put_a(1)
-        put_b(0)
-        put_b(1)
-        for m in range(PACK):
-            round_w(m)
-        for m in range(PACK):
-            quantise_w(m)
-        difference(0, 0)
-        difference(0, 1)
-        put_a(2)
-        difference(1, 0)
-        difference(1, 1)
-        put_b(2)
-        put_a(3)
-        difference(2, 0)
-        put_b(3)
-        difference(2, 1)
+        put_larger(0)
+        put_larger(1)
+        put_smaller(0)
+        put_smaller(1)
+        for u in range(TILES):
+            round_w(u)
+        for u in range(TILES):
+            quantise_w(u)
+        make_z(0, WHOLE)
+        put_larger(2)
+        make_z(1, WHOLE)
+        put_smaller(2)
+        put_larger(3)
+        make_z(2, HALVES[0])
+        put_smaller(3)
+        make_z(2, HALVES[1])
 
         z_codes = keep.tile([P, S], U32, align_bytes=64)
         z_plane = keep.tile([P, S], U8, align_bytes=64)
-        h2 = [keep.tile([P, S], F32, name="h2_%d" % m) for m in range(PACK)]
-        difference(3, 0)
-        difference(3, 1)
-        halves = [slice(0, HALF), slice(HALF, S)]
-        for cols in halves:
+        h2 = [keep.tile([P, S], F32, name="h2_%d" % u) for u in range(TILES)]
+        make_z(3, HALVES[0])
+        make_z(3, HALVES[1])
+        for cols in HALVES:
             nc.vector.quantize_mx(
                 out=z_codes[:, cols].bitcast(FP8X4), scales=z_plane[:, cols],
                 in_=z_grouped[:, cols, :].rearrange("p c t -> p (c t)"),
             )
-        pieces = [(0, halves[0]), (0, halves[1])] + [(m, slice(0, S)) for m in range(1, PACK)]
-        for i, (m, cols) in enumerate(pieces):
-            acc2 = psum.tile([P, cols.stop - cols.start], F32, name="acc2_%d" % i, tag="bank%d" % ((i + PACK) % 8))
-            rows = slice(m * P, (m + 1) * P)
+
+        for i, (u, cols) in enumerate(PIECES):
+            acc2 = psum.tile(
+                [P, cols.stop - cols.start], F32, name="acc2_%d" % i, tag="bank%d" % ((i + len(PIECES)) % BANKS)
+            )
+            rows = slice(u * P, (u + 1) * P)
             nc.tensor.matmul_mx(
                 out=acc2[:], lhsT=w_codes[:, rows].bitcast(FP8X4), lhsT_scale=w_plane[:, rows],
                 rhs=z_codes[:, cols].bitcast(FP8X4), rhs_scale=z_plane[:, cols], start=True, stop=True,
             )
             if i == 0:
-                nc.scalar.copy(h2[m][:, cols], acc2[:])
+                nc.scalar.copy(h2[u][:, cols], acc2[:])
             else:
-                nc.vector.tensor_copy(h2[m][:, cols], acc2[:])
+                nc.vector.tensor_copy(h2[u][:, cols], acc2[:])
 
-        ra2, rb2, res = [], [], []
-        for m in range(PACK):
-            pa2, pb2 = fetch_pair("q%d" % m, h2[m], n4_t, n5_t)
-            ra2_m = keep.tile([P, W], F32, name="ra2_%d" % m)
-            rb2_m = keep.tile([P, W], F32, name="rb2_%d" % m)
-            nc.vector.tensor_tensor(ra2_m[:], pa2[:], pb2[:], ALU.add)
-            nc.vector.tensor_tensor(rb2_m[:], pa2[:], pb2[:], ALU.subtract)
-            ra2.append(ra2_m)
-            rb2.append(rb2_m)
-            res.append(keep.tile([P, S], F32, name="res%d" % m))
-        for m0 in (0, 2):
-            for m in (m0, m0 + 1):
-                nc.scalar.activation(res[m][:].indirect(n4_t[:]), ra2[m][:], COPY, scale=0.75)
-            for m in (m0, m0 + 1):
-                nc.scalar.activation(res[m][:].indirect(n5_t[:]), rb2[m][:], COPY)
-                nc.sync.dma_start(out[m * P:(m + 1) * P, :], res[m][:])
+        sums, differences, result = [], [], []
+        for u in range(TILES):
+            pa2, pb2 = fetch_pair("q%d" % u, h2[u], n4_t, n5_t)
+            sum_u = keep.tile([P, W], F32, name="sum%d" % u)
+            difference_u = keep.tile([P, W], F32, name="difference%d" % u)
+            nc.vector.tensor_tensor(sum_u[:], pa2[:], pb2[:], ALU.add)
+            nc.vector.tensor_tensor(difference_u[:], pa2[:], pb2[:], ALU.subtract)
+            sums.append(sum_u)
+            differences.append(difference_u)
+            result.append(keep.tile([P, S], F32, name="result%d" % u))
+        for first in range(0, TILES, 2):
+            for u in (first, first + 1):
+                nc.scalar.activation(result[u][:].indirect(n4_t[:]), sums[u][:], COPY, scale=0.75)
+            for u in (first, first + 1):
+                nc.scalar.activation(result[u][:].indirect(n5_t[:]), differences[u][:], COPY)
+                nc.sync.dma_start(out[u * P:(u + 1) * P, :], result[u][:])

from contextlib import ExitStack

import concourse.mybir as mybir

K, T, S, N, G, H, W = 512, 2048, 256, 512, 2048, 512, 128
FLOPS = 2 * K * H * S + 2 * H * N * S

F32 = mybir.dt.float32
BF16 = mybir.dt.bfloat16
I32 = mybir.dt.int32
U32 = mybir.dt.uint32
U16 = mybir.dt.uint16
U8 = mybir.dt.uint8
FP8X4 = mybir.dt.float8_e4m3fn_x4
ALU = mybir.AluOpType
COPY = mybir.ActivationFunctionType.Copy

P = 128
PACK = 4
TILES = N // P
LIST_ROWS = 16
BLOCK_ROWS = 8
QUADRANT = 32
LINE_WORDS = 4
BANKS = 8
WHOLE = slice(0, S)
HALVES = (slice(0, S // 2), slice(S // 2, S))
PIECES = ((0, HALVES[0]), (0, HALVES[1]), (1, WHOLE), (2, WHOLE), (3, WHOLE))


def tile_picked_hpqorddhaar_none_p_kernel(
    tc, x_words, x_scales, d_words, d_scales, gn, w1, offs, k1, n1, n2, n3, n4, n5, out
):
    nc = tc.nc
    with ExitStack() as ctx:
        lists = ctx.enter_context(tc.tile_pool(name="lists", bufs=1))
        keep = ctx.enter_context(tc.tile_pool(name="keep", bufs=1))
        psum = ctx.enter_context(tc.psum_pool(name="psum", bufs=1))

        def load_list(name, ap):
            tile = lists.tile(list(ap.shape), U16, name=name)
            nc.sync.dma_start(tile[:], ap)
            return tile

        d_scale_table = keep.tile([P, G], U8, align_bytes=64, tag="scales_then_gain")
        x_scale_table = keep.tile([P, T], U8, align_bytes=64)
        planes = keep.tile([P, H + S], U8, align_bytes=64)
        nc.vector.memset(d_scale_table[:].bitcast(I32), 0)
        nc.vector.memset(x_scale_table[:, 0:T // 2].bitcast(I32), 0)
        nc.gpsimd.memset(x_scale_table[:, T // 2:T].bitcast(I32), 0)
        nc.vector.memset(planes[:].bitcast(I32), 0)

        k1_t = load_list("k1_t", k1)
        offs_t = load_list("offs_t", offs)
        n1_t = load_list("n1_t", n1)
        n2_t = load_list("n2_t", n2)
        nc.sync.dma_start(d_scale_table[:].bitcast(I32)[0:P:BLOCK_ROWS, :], d_scales[0].bitcast(I32))
        n3_t = load_list("n3_t", n3)
        nc.sync.dma_start(x_scale_table[:].bitcast(I32)[0:P:BLOCK_ROWS, :], x_scales[0].bitcast(I32))
        d_table = keep.tile([P, G], I32, align_bytes=64, tag="words_then_w1")
        x_table = keep.tile([P, T], I32, align_bytes=64)
        nc.sync.dma_start(d_table[:], d_words[0].rearrange("p n t -> p (n t)").bitcast(I32))
        nc.sync.dma_start(x_table[:], x_words[0].rearrange("p n t -> p (n t)").bitcast(I32))
        n4_t = load_list("n4_t", n4)
        n5_t = load_list("n5_t", n5)

        picked_scales = keep.tile([P, H + S], U8, align_bytes=64)
        nc.vector.tensor_copy(picked_scales[:, 0:H], d_scale_table[:].indirect(k1_t[:]))
        nc.vector.tensor_copy(picked_scales[:, H:H + S], x_scale_table[:].indirect(offs_t[:]))
        gain = keep.tile([P, PACK], F32, align_bytes=64, tag="scales_then_gain")
        nc.sync.dma_start(gain[:], gn.rearrange("(p t) o -> p (t o)", t=PACK))
        dealt_scales = keep.tile([P, H + S], U8, align_bytes=64)
        nc.vector.tensor_copy(
            dealt_scales[:, 0:H].rearrange("p (t m) -> p t m", t=PACK),
            picked_scales[:, 0:H].rearrange("p (m t) -> p t m", t=PACK),
        )
        nc.vector.tensor_copy(dealt_scales[:, H:H + S].bitcast(I32), picked_scales[:, H:H + S].bitcast(I32))
        for j in range(QUADRANT // BLOCK_ROWS):
            nc.scalar.dma_start(
                planes[:].bitcast(I32)[j:P:QUADRANT, :], dealt_scales[:].bitcast(I32)[BLOCK_ROWS * j:P:QUADRANT, :]
            )

        d_picked = keep.tile([P, H], U32, align_bytes=64)
        nc.vector.tensor_copy(d_picked[:], d_table[:].bitcast(U32).indirect(k1_t[:]))
        d_dealt = keep.tile([P, H], U32, align_bytes=64)
        nc.vector.tensor_copy(
            d_dealt[:].rearrange("p (t b i) -> p b t i", t=PACK, i=LINE_WORDS),
            d_picked[:].rearrange("p (b i t) -> p b t i", t=PACK, i=LINE_WORDS),
        )
        x_picked = keep.tile([P, S], U32, align_bytes=64)
        nc.vector.tensor_copy(x_picked[:], x_table[:].bitcast(U32).indirect(offs_t[:]))

        w_raw = keep.tile([P, PACK, N], F32, align_bytes=64, tag="words_then_w1")
        nc.sync.dma_start(w_raw[:], w1.rearrange("(p t) n -> p t n", t=PACK))

        h = [keep.tile([P, S], F32, name="h%d" % t) for t in range(PACK)]
        for i, (t, cols) in enumerate(PIECES):
            acc = psum.tile([P, cols.stop - cols.start], F32, name="acc%d" % i, tag="bank%d" % i)
            rows = slice(t * P, (t + 1) * P)
            nc.tensor.matmul_mx(
                out=acc[:], lhsT=d_dealt[:, rows].bitcast(FP8X4), lhsT_scale=planes[:, rows],
                rhs=x_picked[:, cols].bitcast(FP8X4), rhs_scale=planes[:, H + cols.start:H + cols.stop],
                start=True, stop=True,
            )
            nc.vector.tensor_scalar(h[t][:, cols], acc[:], 0.0625, None, ALU.mult)

        def fetch_pair(name, window, first, second):
            a = keep.tile([P, W], F32, name=name + "a")
            b = keep.tile([P, W], F32, name=name + "b")
            nc.scalar.activation(a[:], window[:].indirect(first[:]), COPY)
            nc.scalar.activation(b[:], window[:].indirect(second[:]), COPY)
            return a, b

        ra, rb, dt = [], [], []
        for t in range(PACK):
            pa, pb = fetch_pair("p%d" % t, h[t], n1_t, n2_t)
            ra_t = keep.tile([P, W], F32, name="ra%d" % t)
            rb_t = keep.tile([P, W], F32, name="rb%d" % t)
            nc.vector.tensor_tensor(ra_t[:], pa[:], pb[:], ALU.max)
            nc.vector.tensor_tensor(rb_t[:], pa[:], pb[:], ALU.min)
            ra.append(ra_t)
            rb.append(rb_t)
            dt.append(keep.tile([P, 2 * S if t < PACK // 2 else S], F32, name="dt%d" % t))

        z_grouped = keep.tile([P, S, PACK], BF16, align_bytes=64)
        partner = [keep.tile([P, S], F32, name="partner%d" % t) for t in range(PACK)]

        def put_larger(t):
            nc.scalar.activation(dt[t][:].indirect(n1_t[:]), ra[t][:], COPY)

        def put_smaller(t):
            nc.scalar.activation(dt[t][:].indirect(n2_t[:]), rb[t][:], COPY)

        def make_z(t, cols):
            entries = n3_t[:, cols.start // LIST_ROWS:cols.stop // LIST_ROWS]
            nc.scalar.activation(partner[t][:, cols], dt[t][:].indirect(entries), COPY, scale=gain[:, t:t + 1])
            nc.vector.scalar_tensor_tensor(
                z_grouped[:, cols, t], dt[t][:, cols], gain[:, t:t + 1], partner[t][:, cols], ALU.mult, ALU.subtract
            )

        w_codes = keep.tile([P, N], U32, align_bytes=64)
        w_plane = keep.tile([P, N], U8, align_bytes=64)
        w_grouped = keep.tile([P, N, PACK], BF16, align_bytes=64)

        def round_w(u):
            cols = slice(u * P, (u + 1) * P)
            nc.vector.tensor_copy(
                w_grouped[:, cols, :].rearrange("p (c i) t -> p c t i", i=LINE_WORDS),
                w_raw[:, :, cols].rearrange("p t (c i) -> p c t i", i=LINE_WORDS),
            )

        def quantise_w(u):
            cols = slice(u * P, (u + 1) * P)
            nc.vector.quantize_mx(
                out=w_codes[:, cols].bitcast(FP8X4), scales=w_plane[:, cols],
                in_=w_grouped[:, cols, :].rearrange("p c t -> p (c t)"),
            )

        put_larger(0)
        put_larger(1)
        put_smaller(0)
        put_smaller(1)
        for u in range(TILES):
            round_w(u)
        for u in range(TILES):
            quantise_w(u)
        make_z(0, WHOLE)
        put_larger(2)
        make_z(1, WHOLE)
        put_smaller(2)
        put_larger(3)
        make_z(2, HALVES[0])
        put_smaller(3)
        make_z(2, HALVES[1])

        z_codes = keep.tile([P, S], U32, align_bytes=64)
        z_plane = keep.tile([P, S], U8, align_bytes=64)
        h2 = [keep.tile([P, S], F32, name="h2_%d" % u) for u in range(TILES)]
        make_z(3, HALVES[0])
        make_z(3, HALVES[1])
        for cols in HALVES:
            nc.vector.quantize_mx(
                out=z_codes[:, cols].bitcast(FP8X4), scales=z_plane[:, cols],
                in_=z_grouped[:, cols, :].rearrange("p c t -> p (c t)"),
            )

        for i, (u, cols) in enumerate(PIECES):
            acc2 = psum.tile(
                [P, cols.stop - cols.start], F32, name="acc2_%d" % i, tag="bank%d" % ((i + len(PIECES)) % BANKS)
            )
            rows = slice(u * P, (u + 1) * P)
            nc.tensor.matmul_mx(
                out=acc2[:], lhsT=w_codes[:, rows].bitcast(FP8X4), lhsT_scale=w_plane[:, rows],
                rhs=z_codes[:, cols].bitcast(FP8X4), rhs_scale=z_plane[:, cols], start=True, stop=True,
            )
            if i == 0:
                nc.scalar.copy(h2[u][:, cols], acc2[:])
            else:
                nc.vector.tensor_copy(h2[u][:, cols], acc2[:])

        sums, differences, result = [], [], []
        for u in range(TILES):
            pa2, pb2 = fetch_pair("q%d" % u, h2[u], n4_t, n5_t)
            sum_u = keep.tile([P, W], F32, name="sum%d" % u)
            difference_u = keep.tile([P, W], F32, name="difference%d" % u)
            nc.vector.tensor_tensor(sum_u[:], pa2[:], pb2[:], ALU.add)
            nc.vector.tensor_tensor(difference_u[:], pa2[:], pb2[:], ALU.subtract)
            sums.append(sum_u)
            differences.append(difference_u)
            result.append(keep.tile([P, S], F32, name="result%d" % u))
        for first in range(0, TILES, 2):
            for u in (first, first + 1):
                nc.scalar.activation(result[u][:].indirect(n4_t[:]), sums[u][:], COPY, scale=0.75)
            for u in (first, first + 1):
                nc.scalar.activation(result[u][:].indirect(n5_t[:]), differences[u][:], COPY)
                nc.sync.dma_start(out[u * P:(u + 1) * P, :], result[u][:])
